import numpy as np
import ml_dtypes


def mxq(x, axis, fmt="e4m3"):
    dtype, down = {"e4m3": (ml_dtypes.float8_e4m3fn, 7), "e5m2": (ml_dtypes.float8_e5m2, 14)}[fmt]
    v = np.moveaxis(np.asarray(x, np.float32).astype(ml_dtypes.bfloat16).astype(np.float64), axis, -1)
    blocks = v.reshape(v.shape[:-1] + (-1, 32))
    amax = np.abs(blocks).max(-1, keepdims=True)
    byte = np.maximum(np.where(amax > 0, np.frexp(amax)[1] - 1 + 127, 0) - down, 1)
    scale = np.exp2(byte - 127.0)
    codes = (blocks / scale).astype(np.float32).astype(dtype).astype(np.float64)
    return np.moveaxis((codes * scale).reshape(v.shape), -1, axis)


WIDE = False


def mx_kscale(k):
    if not WIDE:
        return np.ones(k)
    levels = np.array([10, -10, 5, -5, 0])
    if k % 512:
        return np.exp2(np.random.permutation(np.resize(levels, k // 32))).repeat(32)
    a = np.empty((k // 512, 16))
    for p in range(k // 512):
        a[p, :8] = np.random.permutation(np.resize(levels, 8))
        for g in range(8):
            far = levels[np.abs(levels - a[p, g]) >= 10]
            a[p, g + 8] = far[np.random.randint(len(far))]
    return np.exp2(a.ravel()).repeat(32)


BF16 = ml_dtypes.bfloat16


def bf(x):
    return np.asarray(x, np.float32).astype(BF16)


def f64(x):
    return np.asarray(x).astype(np.float64)


N, K, C = 96, 16, 512


def leaky(r):
    return np.maximum(r, 0.2 * r)


def neighbour_softmax(logits):
    m = np.max(logits, axis=1, keepdims=True)
    e = np.exp(logits - m)
    return e / np.sum(e, axis=1, keepdims=True)


def draw0():
    s, t = mx_kscale(C), mx_kscale(C)
    return {
        "xn": bf(np.random.standard_normal((N, K, C)) * s),
        "q": bf(np.random.standard_normal((N, C))),
        "delta": bf(np.random.standard_normal((N, K, C)) * 0.7),
        "wk": bf(np.random.standard_normal((C, C)) / np.sqrt(C) / s[:, None]),
        "wv": bf(np.random.standard_normal((C, C)) / np.sqrt(C) / s[:, None]),
        "gain": bf((1.0 + 0.1 * np.random.standard_normal(C)) * t),
        "wg": bf(1.5 * np.random.standard_normal((C, C)) / np.sqrt(C) / t[:, None]),
    }


def core(xn, q, delta, wk, wv, gain, wg):
    d = f64(delta)
    xq = mxq(f64(xn), 2, "e4m3")
    kx = xq @ mxq(f64(wk), 0, "e4m3")
    vx = xq @ mxq(f64(wv), 0, "e4m3")
    r = f64(q)[:, None, :] - kx + d
    h = leaky(r) * f64(gain)
    logits = mxq(h, 2, "e4m3") @ mxq(f64(wg), 0, "e4m3")
    a = neighbour_softmax(logits)
    return np.sum(a * (vx + d), axis=1)


def e4m3fn_bytes(y):
    return np.clip(np.asarray(y, np.float64), -448.0, 448.0).astype(np.float32).astype(ml_dtypes.float8_e4m3fn).view(np.uint8)


def e4m3fn_values(b):
    return np.asarray(b, np.uint8).view(ml_dtypes.float8_e4m3fn).astype(np.float64)


def setup_inputs():
    d = draw0()
    x0 = np.asarray(d['xn']).astype(np.float64)
    s = (np.max(np.abs(x0), axis=(0, 1), keepdims=True) / 448.0).astype(np.float32)
    out = {}
    for k, v in d.items():
        if k == 'xn':
            out['xn_bytes'] = e4m3fn_bytes(x0 / s.astype(np.float64))
            out['xn_scale'] = s
        else:
            out[k] = v
    return out


def reference(xn_bytes, xn_scale, q, delta, wk, wv, gain, wg):
    return core(e4m3fn_values(xn_bytes) * xn_scale.astype(np.float64), q, delta, wk, wv, gain, wg)

from contextlib import ExitStack

import concourse.mybir as mybir
from concourse.masks import make_identity

N, K, C = 96, 16, 512
FLOPS = 3 * 2 * N * K * C * C

P = 128
NT = 4
CH = 3
PTS = N // CH
TOK = PTS * K
XR = 4
DT = 5
DPT = 7
DROW = DPT * K

F32 = mybir.dt.float32
BF16 = mybir.dt.bfloat16
U32 = mybir.dt.uint32
U8 = mybir.dt.uint8
FP8 = mybir.dt.float8_e4m3fn
FP8X4 = mybir.dt.float8_e4m3fn_x4
ALU = mybir.AluOpType
ACT = mybir.ActivationFunctionType
AX = mybir.AxisListType


def tile_pointtransformervectorattention_kernel(
    tc, xn_bytes, xn_scale, q, delta, wk, wv, gain, wg, out
):
    nc = tc.nc
    with ExitStack() as ctx:
        const = ctx.enter_context(tc.tile_pool(name="const", bufs=1))
        work = ctx.enter_context(tc.tile_pool(name="work", bufs=2))
        ring = ctx.enter_context(tc.psum_pool(name="ring", bufs=7))
        sums = ctx.enter_context(tc.psum_pool(name="sums", bufs=1))
        ctx.enter_context(tc.manual_schedule())

        sc = const.tile([P, NT], F32, name="sc")
        gcol = const.tile([P, NT], BF16, name="gcol")
        xraw = [const.tile([P, XR, C], U8, name=f"xraw{c}") for c in range(CH)]
        wraw = {w: const.tile([P, NT, C], BF16, name=f"raw_{w}") for w in ("wk", "wv", "wg")}
        dt = const.tile([P, CH * DT, C], BF16, name="dt")
        delta2 = delta.rearrange("n j c -> (n j) c")
        x2 = xn_bytes.rearrange("n j c -> (n j) c")

        def load_x(c):
            nc.sync.dma_start(
                out=xraw[c][:],
                in_=x2[c * TOK : (c + 1) * TOK, :].rearrange("(p i) k -> p i k", i=XR),
            )

        def load_w(name, src):
            nc.sync.dma_start(out=wraw[name][:], in_=src.rearrange("(p j) c -> p j c", j=NT))

        def load_d(c):
            s0 = c * DT
            nc.sync.dma_start(
                out=dt[0:DROW, s0 : s0 + 4, :],
                in_=delta2[c * TOK : c * TOK + 4 * DROW, :].rearrange("(i r) c -> r i c", r=DROW),
            )
            nc.sync.dma_start(out=dt[0:DROW, s0 + 4, :], in_=delta2[(c + 1) * TOK - DROW : (c + 1) * TOK, :])
            nc.sync.dma_start(
                out=dt[DROW : DROW + DPT, s0 : s0 + 4, :],
                in_=q[c * PTS : c * PTS + 4 * DPT, :].rearrange("(i r) c -> r i c", r=DPT),
            )
            nc.sync.dma_start(out=dt[DROW : DROW + DPT, s0 + 4, :], in_=q[(c + 1) * PTS - DPT : (c + 1) * PTS, :])

        nc.scalar.dma_start(out=sc[:], in_=xn_scale.rearrange("a b (p t) -> p (a b t)", t=NT))
        nc.scalar.dma_start(out=gcol[:], in_=gain.rearrange("(p t) -> p t", t=NT))
        nc.vector.memset(dt[96:P, :, :].rearrange("p s c -> p (s c)").bitcast(U32), 0)
        load_x(0)
        load_w("wk", wk)
        load_d(0)
        load_x(1)
        load_w("wv", wv)
        load_w("wg", wg)
        load_d(1)
        load_x(2)
        load_d(2)

        warm = const.tile([P, 1], F32, name="warm")
        nc.vector.memset(warm[:], 0.0)
        nc.scalar.activation(out=warm[:], in_=warm[:], func=ACT.Exp)
        identf = const.tile([P, P], F32, name="identf")
        make_identity(nc, identf[:])
        identb = const.tile([P, P], BF16, name="identb")
        make_identity(nc, identb[:])
        sel = const.tile([P, DROW], BF16, name="sel")
        nc.vector.tensor_tensor(
            out=sel[:].rearrange("p (a j) -> p a j", j=K),
            in0=identb[:, 0:DROW].rearrange("p (a j) -> p a j", j=K),
            in1=identb[:, DROW : DROW + DPT].unsqueeze(2).to_broadcast([P, DPT, K]),
            op=ALU.add,
        )
        sgn = const.tile([P, NT], F32, name="sgn")
        ag = const.tile([P, NT], F32, name="ag")
        ng = const.tile([P, NT], F32, name="ng")

        def ps_bank(shape, dtype):
            b = ring.tile(shape, dtype, tag="b", name="b")
            return b

        scb = const.tile([P, C], F32, name="scb")
        scps = ps_bank([P, NT, P], F32)
        for t in range(NT):
            nc.tensor.transpose(scps[:, t, :], sc[:, t : t + 1].to_broadcast([P, P]), identf[:])
        nc.vector.tensor_copy(
            out=scb[:].rearrange("p (m t) -> p m t", t=NT), in_=scps[:].rearrange("p t m -> p m t")
        )

        xb, xg, xcode, xscl = {}, {}, {}, {}
        Dg, dTs, kx, vx, lg, ys, hb, hcode, hscl, zs, vps, ms = {}, {}, {}, {}, {}, {}, {}, {}, {}, {}, {}, {}
        wgrp, wcode, wscl = {}, {}, {}
        for w in ("wk", "wv", "wg"):
            wgrp[w] = const.tile([P, C, NT], BF16, name=f"grp_{w}", align_bytes=64)
            wcode[w] = const.tile([P, C], U32, name=f"code_{w}", align_bytes=64)
            wscl[w] = const.tile([P, C], U8, name=f"scl_{w}", align_bytes=64)
        for c in range(CH):
            xcode[c] = const.tile([P, TOK], U32, name=f"xcode{c}", align_bytes=64)
            xscl[c] = const.tile([P, TOK], U8, name=f"xscl{c}", align_bytes=64)

        def quant(codes, scl, src):
            nc.vector.quantize_mx(out=codes[:].bitcast(FP8X4), scales=scl[:], in_=src[:].rearrange("p c t -> p (c t)"))

        def x_product(c, rows):
            if c not in xb:
                t_xb = work.tile([P, XR, C], BF16, tag="xb", name="t_xb")
                xb[c] = t_xb
            for i in rows:
                nc.vector.tensor_tensor(
                    out=xb[c][:, i, :], in0=xraw[c][:, i, :].bitcast(FP8), in1=scb[:], op=ALU.mult
                )

        def x_turn(c, half):
            if c not in xg:
                t_xg = work.tile([P, TOK, NT], BF16, tag="xg", name="t_xg", align_bytes=64)
                xg[c] = t_xg
            xt = ps_bank([P, 4, P], F32)
            for i in range(2):
                words = xb[c][:, 2 * half + i, :].bitcast(F32)
                for u in range(2):
                    nc.tensor.transpose(xt[:, 2 * i + u, :], words[:, u : C // 2 : 2], identf[:])
            dst = xg[c][:].rearrange("p c t -> p (c t)").bitcast(F32).rearrange("p (m b r) -> p b m r", b=2, r=4)
            nc.scalar.copy(out=dst[:, half], in_=xt[:].rearrange("p r m -> p m r"))

        def d_sum(c):
            t_dg = work.tile([P, NT, TOK], F32, tag="dg", name="t_dg")
            Dg[c] = t_dg
            for t in range(NT):
                dp = ps_bank([P, TOK], F32)
                for i in range(DT):
                    s = c * DT + i
                    lo = 0 if i < 4 else 3 * K
                    nc.tensor.matmul(
                        out=dp[:, i * DROW : i * DROW + DROW - lo],
                        lhsT=dt[:, s, t:C:NT],
                        rhs=sel[:, lo:DROW],
                        start=True,
                        stop=True,
                    )
                nc.scalar.activation(out=t_dg[:, t, :], in_=dp[:], func=ACT.Copy, scale=ag[:, t : t + 1])

        def d_turn(c):
            t_dt = work.tile([P, NT, TOK], BF16, tag="dtt", name="t_dt")
            dTs[c] = t_dt
            for t in range(NT):
                dp = ps_bank([P, DT, P], BF16)
                for i in range(DT):
                    nc.tensor.transpose(dp[:, i, :], dt[:, c * DT + i, t * P : (t + 1) * P], identb[:])
                nc.scalar.copy(
                    out=t_dt[:, t, 0 : 4 * DROW].rearrange("p (i r) -> p i r", i=4), in_=dp[:, 0:4, 0:DROW]
                )
                nc.scalar.copy(out=t_dt[:, t, 4 * DROW : TOK], in_=dp[:, 4, 3 * K : DROW])

        def mm(store, c, w, codes, scl):
            store[c] = []
            for t in range(NT):
                acc = ps_bank([P, TOK], F32)
                cols = slice(t * P, (t + 1) * P)
                nc.tensor.matmul_mx(
                    out=acc[:],
                    lhsT=wcode[w][:, cols].bitcast(FP8X4),
                    lhsT_scale=wscl[w][:, cols],
                    rhs=codes[:].bitcast(FP8X4),
                    rhs_scale=scl[:],
                    start=True,
                    stop=True,
                )
                store[c].append(acc)

        def r_step(c):
            t_y = work.tile([P, NT, TOK], F32, tag="y", name="t_y")
            ys[c] = t_y
            for t in range(NT):
                nc.vector.scalar_tensor_tensor(
                    out=t_y[:, t, :], in0=kx[c][t][:], scalar=ng[:, t : t + 1], in1=Dg[c][:, t, :],
                    op0=ALU.mult, op1=ALU.add,
                )

        def leaky(c):
            t_hb = work.tile([P, TOK, NT], BF16, tag="hb", name="t_hb", align_bytes=64)
            hb[c] = t_hb
            for h in range(2):
                cols = slice(h * TOK // 2, (h + 1) * TOK // 2)
                yv = ys[c][:, :, cols].rearrange("p t n -> p n t")
                nc.vector.scalar_tensor_tensor(
                    out=t_hb[:, cols, :], in0=yv, scalar=0.2, in1=yv, op0=ALU.mult, op1=ALU.max
                )

        def h_quant(c):
            t_hc = work.tile([P, TOK], U32, tag="hc", name="t_hc", align_bytes=64)
            t_hs = work.tile([P, TOK], U8, tag="hs", name="t_hs", align_bytes=64)
            hcode[c], hscl[c] = t_hc, t_hs
            quant(t_hc, t_hs, hb[c])

        def v_add(c):
            t_vp = work.tile([P, K, NT, PTS], F32, tag="vp", name="t_vp")
            vps[c] = t_vp
            for t in range(NT):
                nc.vector.tensor_tensor(
                    out=t_vp[:, :, t, :],
                    in0=vx[c][t][:].rearrange("p (n j) -> p j n", j=K),
                    in1=dTs[c][:, t, :].rearrange("p (n j) -> p j n", j=K),
                    op=ALU.add,
                )

        def soft(c):
            t_z = work.tile([P, K, NT, PTS], F32, tag="z", name="t_z")
            t_m = work.tile([P, NT, PTS], F32, tag="m", name="t_m")
            zs[c] = t_z

            def top(t):
                nc.vector.tensor_reduce(
                    out=t_m[:, t, :], in_=lg[c][t][:].rearrange("p (n j) -> p n j", j=K), axis=AX.X, op=ALU.max
                )

            def sub_exp(t):
                nc.vector.tensor_tensor(
                    out=t_z[:, :, t, :],
                    in0=lg[c][t][:].rearrange("p (n j) -> p j n", j=K),
                    in1=t_m[:, t, :].unsqueeze(1).to_broadcast([P, K, PTS]),
                    op=ALU.subtract,
                )
                nc.scalar.activation(out=t_z[:, :, t, :], in_=t_z[:, :, t, :], func=ACT.Exp)

            top(0)
            for t in range(NT):
                if t + 1 < NT:
                    top(t + 1)
                sub_exp(t)

        def weigh(c, t, eng):
            eng.tensor_tensor(out=vps[c][:, :, t, :], in0=vps[c][:, :, t, :], in1=zs[c][:, :, t, :], op=ALU.mult)

        def sum_up(c):
            su = sums.tile([P, 2, P], F32, tag="su", name="su")
            for part, src in ((0, zs[c]), (1, vps[c])):
                for j in range(K):
                    nc.tensor.matmul(
                        out=su[:, part, :],
                        lhsT=src[:, j, :, :].rearrange("p t n -> p (t n)"),
                        rhs=identf[:],
                        is_transpose=True,
                        start=(j == 0),
                        stop=(j == K - 1),
                    )
            t_r = work.tile([P, P], F32, tag="r", name="t_r")
            t_o = work.tile([P, P], F32, tag="o", name="t_o")
            nc.vector.reciprocal(out=t_r[:], in_=su[:, 0, :])
            nc.vector.tensor_tensor(out=t_o[:], in0=su[:, 1, :], in1=t_r[:], op=ALU.mult)
            for t in range(NT):
                nc.sync.dma_start(
                    out=out[c * PTS : (c + 1) * PTS, t * P : (t + 1) * P], in_=t_o[t * PTS : (t + 1) * PTS, :]
                )

        def w_inter(w, src, eng_copy):
            eng_copy(
                out=wgrp[w][:].rearrange("p (c i) t -> p c t i", i=4),
                in_=src[:].rearrange("p t (c i) -> p c t i", i=4),
            )

        x_product(0, (0, 1))
        x_turn(0, 0)
        x_product(0, (2, 3))
        x_turn(0, 1)
        nc.vector.tensor_scalar(out=sgn[:], in0=gcol[:], scalar1=0.0, scalar2=2.0, op0=ALU.is_ge, op1=ALU.mult)
        nc.vector.tensor_scalar(out=sgn[:], in0=sgn[:], scalar1=-1.0, scalar2=None, op0=ALU.add)
        nc.vector.tensor_tensor(out=ag[:], in0=gcol[:], in1=sgn[:], op=ALU.mult)
        nc.vector.tensor_scalar(out=ng[:], in0=ag[:], scalar1=-1.0, scalar2=None, op0=ALU.mult)
        d_sum(0)
        for t in range(NT):
            nc.vector.tensor_copy(
                out=wgrp["wk"][:, t * P : (t + 1) * P, :],
                in_=wraw["wk"][:].rearrange("p j (m t) -> p t m j", t=NT)[:, t],
            )
        x_product(1, (0, 1))
        quant(xcode[0], xscl[0], xg[0])
        quant(wcode["wk"], wscl["wk"], wgrp["wk"])
        x_product(1, (2, 3))
        mm(kx, 0, "wk", xcode[0], xscl[0])
        w_inter("wv", wraw["wv"], nc.scalar.copy)
        x_turn(1, 0)
        x_turn(1, 1)
        r_step(0)
        quant(xcode[1], xscl[1], xg[1])
        d_turn(0)
        leaky(0)
        quant(wcode["wv"], wscl["wv"], wgrp["wv"])
        h_quant(0)
        mm(vx, 0, "wv", xcode[0], xscl[0])
        wsg = const.tile([P, NT, C], BF16, name="wsg")
        for j in range(NT):
            nc.gpsimd.tensor_scalar(
                out=wsg[:, j, :], in0=wraw["wg"][:, j, :], scalar1=sgn[:, j : j + 1], scalar2=0.0,
                op0=ALU.mult, op1=ALU.add,
            )
        w_inter("wg", wsg, nc.scalar.copy)
        v_add(0)
        quant(wcode["wg"], wscl["wg"], wgrp["wg"])
        mm(lg, 0, "wg", hcode[0], hscl[0])
        x_product(2, (0, 1))
        d_sum(1)
        mm(kx, 1, "wk", xcode[1], xscl[1])
        soft(0)
        r_step(1)
        for t in range(NT):
            weigh(0, t, nc.gpsimd)
        x_turn(2, 0)
        x_product(2, (2, 3))
        x_turn(2, 1)
        leaky(1)
        d_turn(1)
        mm(vx, 1, "wv", xcode[1], xscl[1])
        quant(xcode[2], xscl[2], xg[2])
        h_quant(1)
        v_add(1)
        mm(lg, 1, "wg", hcode[1], hscl[1])
        sum_up(0)
        d_sum(2)
        mm(kx, 2, "wk", xcode[2], xscl[2])
        soft(1)
        r_step(2)
        for t in range(NT):
            weigh(1, t, nc.gpsimd)
        leaky(2)
        d_turn(2)
        mm(vx, 2, "wv", xcode[2], xscl[2])
        h_quant(2)
        mm(lg, 2, "wg", hcode[2], hscl[2])
        v_add(2)
        sum_up(1)
        soft(2)
        for t in range(NT):
            weigh(2, t, nc.gpsimd if t < 2 else nc.vector)
        sum_up(2)
